import numpy as np
import ml_dtypes


def mxq(x, axis, fmt="e4m3"):
    dtype, down = {"e4m3": (ml_dtypes.float8_e4m3fn, 7), "e5m2": (ml_dtypes.float8_e5m2, 14)}[fmt]
    v = np.moveaxis(np.asarray(x, np.float32).astype(ml_dtypes.bfloat16).astype(np.float64), axis, -1)
    blocks = v.reshape(v.shape[:-1] + (-1, 32))
    amax = np.abs(blocks).max(-1, keepdims=True)
    byte = np.maximum(np.where(amax > 0, np.frexp(amax)[1] - 1 + 127, 0) - down, 1)
    scale = np.exp2(byte - 127.0)
    codes = (blocks / scale).astype(np.float32).astype(dtype).astype(np.float64)
    return np.moveaxis((codes * scale).reshape(v.shape), -1, axis)


WIDE = False


def mx_kscale(k):
    if not WIDE:
        return np.ones(k)
    levels = np.array([30, -30])
    if k % 512:
        return np.exp2(np.random.permutation(np.resize(levels, k // 32))).repeat(32)
    a = np.empty((k // 512, 16))
    for p in range(k // 512):
        a[p, :8] = np.random.permutation(np.resize(levels, 8))
        for g in range(8):
            far = levels[np.abs(levels - a[p, g]) >= 10]
            a[p, g + 8] = far[np.random.randint(len(far))]
    return np.exp2(a.ravel()).repeat(32)


def f64(x):
    return np.asarray(x).astype(np.float64)


def striped(idx):
    return np.tile(np.asarray(idx).reshape(-1, 16).T, (8, 1)).astype(np.uint16)


def unstriped(offs):
    return offs[:16].T.reshape(-1).astype(np.int64)


E2M1 = np.array([0.0, 0.5, 1.0, 1.5, 2.0, 3.0, 4.0, 6.0, -0.0, -0.5, -1.0, -1.5, -2.0, -3.0, -4.0, -6.0])


def pack_weight(w, fmt):
    k, n = w.shape
    w = f64(np.asarray(w, np.float32).astype(ml_dtypes.bfloat16)).reshape(k // 32, 32, n)
    amax = np.abs(w).max(1)
    if fmt == "e4m3":
        byte = np.frexp(amax)[1] - 1 + 127 - 7
    else:
        mant, ex = np.frexp(amax / 6.0)
        byte = np.where(mant > 0.5, ex, ex - 1) + 127
    byte = np.clip(np.where(amax > 0, byte, 1), 1, 254)
    scaled = (w * np.exp2(127.0 - byte)[:, None, :]).reshape(k, n).astype(np.float32)
    by_word = np.ascontiguousarray(scaled.reshape(k // 512, 128, 4, n).transpose(0, 1, 3, 2))
    if fmt == "e4m3":
        words = by_word.astype(ml_dtypes.float8_e4m3fn).view(np.uint8)
    else:
        c = by_word.astype(ml_dtypes.float4_e2m1fn).view(np.uint8) & 0xF
        words = (c[..., 0::2] | (c[..., 1::2] << 4)).reshape(k // 512, 128, 2 * n)
    return np.ascontiguousarray(words), np.ascontiguousarray(byte.astype(np.uint8).reshape(k // 512, 16, n))


def unpack_weight(words, scales, fmt):
    g, _, n = scales.shape
    words = np.ascontiguousarray(words).reshape(g, 128, n, -1)
    if fmt == "e4m3":
        vals = words.view(ml_dtypes.float8_e4m3fn).astype(np.float64)
    else:
        nib = np.empty((g, 128, n, 4), np.uint8)
        nib[..., 0::2] = words & 0xF
        nib[..., 1::2] = words >> 4
        vals = E2M1[nib]
    vals = vals * np.repeat(np.exp2(scales.astype(np.float64) - 127.0), 8, axis=1)[..., None]
    return vals.transpose(0, 1, 3, 2).reshape(g * 512, n)


def sigmoid(v):
    return 1.0 / (1.0 + np.exp(-v))


def sgn(shape):
    return np.random.uniform(0.5, 2.0, shape) * np.where(np.random.standard_normal(shape) < 0, -1.0, 1.0)


K, T, J, R, F, Z, O, N, E = 512, 1024, 256, 512, 512, 1024, 128, 256, 1024


def setup_inputs():
    n = np.random.standard_normal
    idx = np.random.permutation(T)[:J]
    idx2 = np.random.permutation(Z)[:J]
    idx3 = np.random.permutation(J)[:O]
    idx4 = np.random.permutation(J)[:O]
    idx5 = np.random.permutation(J)[:O]
    idx6 = np.random.permutation(E)[:O]
    fk = mx_kscale(K)
    ff = mx_kscale(F)
    fr = mx_kscale(R)
    xtp = pack_weight(n((K, T)) / fk[:, None], "e2m1")
    xop = pack_weight(n((F, Z)) / ff[:, None], "e4m3")
    wp = pack_weight(n((K, R)) * 1 / np.sqrt(K) * fk[:, None], "e4m3")
    w0p = pack_weight(n((F, R)) * 1 / np.sqrt(F) * ff[:, None], "e2m1")
    wbp = pack_weight(n((R, N)) * 1 / np.sqrt(R) / fr[:, None], "e2m1")
    return {
        "xt_words": xtp[0],
        "xt_scales": xtp[1],
        "xo_words": xop[0],
        "xo_scales": xop[1],
        "w_words": wp[0],
        "w_scales": wp[1],
        "w0_words": w0p[0],
        "w0_scales": w0p[1],
        "sa": (np.random.uniform(0.5, 1.6, (R, 1)) * fr[:, None]).astype(np.float32),
        "sb": (np.random.uniform(0.5, 1.6, (R, 1)) * fr[:, None]).astype(np.float32),
        "sg": (sgn((R, 1))).astype(np.float32),
        "bg": (np.random.uniform(-2.0, 2.0, (R, 1))).astype(np.float32),
        "wb_words": wbp[0],
        "wb_scales": wbp[1],
        "offs": striped(idx),
        "offs2": striped(idx2),
        "offs3": striped(idx3),
        "offs4": striped(idx4),
        "offs5": striped(idx5),
        "offs6": striped(idx6),
    }


def reference(xt_words, xt_scales, xo_words, xo_scales, w_words, w_scales, w0_words, w0_scales, sa, sb, sg, bg, wb_words, wb_scales, offs, offs2, offs3, offs4, offs5, offs6):
    idx = unstriped(offs)
    idx2 = unstriped(offs2)
    idx3 = unstriped(offs3)
    idx4 = unstriped(offs4)
    idx5 = unstriped(offs5)
    idx6 = unstriped(offs6)
    xtu = unpack_weight(xt_words, xt_scales, "e2m1")
    xou = unpack_weight(xo_words, xo_scales, "e4m3")
    wu = unpack_weight(w_words, w_scales, "e4m3")
    w0u = unpack_weight(w0_words, w0_scales, "e2m1")
    wbu = unpack_weight(wb_words, wb_scales, "e2m1")
    xtidxg = xtu[:, idx]
    xoidx2g = xou[:, idx2]
    a = wu.T @ xtidxg + w0u.T @ xoidx2g
    hid = np.abs(a[:, idx3] * f64(sa) - a[:, idx4] * f64(sb)) * sigmoid(a[:, idx5] * f64(sg) + f64(bg))
    hidq = mxq(hid, 0, "e5m2")
    p = wbu.T @ hidq
    y = np.zeros((N, E))
    y[:, idx6] = p
    return y

@@ -1,0 +1,193 @@
+from contextlib import ExitStack
+
+import concourse.mybir as mybir
+
+K, T, J, R, F, Z, O, N, E = 512, 1024, 256, 512, 512, 1024, 128, 256, 1024
+FLOPS = 2 * (K * R * J + F * R * J + R * N * O)
+
+F32 = mybir.dt.float32
+BF16 = mybir.dt.bfloat16
+I32 = mybir.dt.int32
+U32 = mybir.dt.uint32
+U16 = mybir.dt.uint16
+U8 = mybir.dt.uint8
+E4M3 = mybir.dt.float8_e4m3fn_x4
+E5M2 = mybir.dt.float8_e5m2_x4
+E2M1 = mybir.dt.float4_e2m1fn_x4
+ACT = mybir.ActivationFunctionType
+ALU = mybir.AluOpType
+
+P = 128
+PACK = 4
+
+
+def stage_scales(queue, staged, scales):
+    queue.dma_start(out=staged[:], in_=scales[0].bitcast(I32).rearrange("(q r) c -> r q c", r=4))
+
+
+def load_scales(queue, plane, scales):
+    for q in range(4):
+        queue.dma_start(out=plane[32 * q : 32 * q + 4, :].bitcast(I32), in_=scales[0, 4 * q : 4 * q + 4, :].bitcast(I32))
+
+
+def deal(copy, dealt, raw, run, slots):
+    copy(
+        out=dealt.rearrange("p (t b i) -> p b t i", t=PACK, i=run)[:, :, slots, :],
+        in_=raw.rearrange("p (b i t) -> p b t i", t=PACK, i=run)[:, :, slots, :],
+    )
+
+
+def tile_list_gatedlarger_bank_one_scattered_kernel(
+    tc, xt_words, xt_scales, xo_words, xo_scales, w_words, w_scales, w0_words, w0_scales,
+    sa, sb, sg, bg, wb_words, wb_scales, offs, offs2, offs3, offs4, offs5, offs6, out,
+):
+    nc = tc.nc
+    with ExitStack() as ctx:
+        pool = ctx.enter_context(tc.tile_pool(name="held", bufs=1))
+        psum = ctx.enter_context(tc.psum_pool(name="psum", bufs=1))
+
+        def tile(name, shape, dtype):
+            return pool.tile(shape, dtype, name=name, align_bytes=64)
+
+        def load_list(name, source):
+            t = tile(name, list(source.shape), U16)
+            nc.sync.dma_start(t[:], source)
+            return t
+
+        def load_rows(queue, name, source):
+            t = tile(name, [P, PACK], F32)
+            queue.dma_start(out=t[:], in_=source.rearrange("(p t) o -> p (t o)", t=PACK))
+            return t
+
+        xt_s = tile("xt_s", [P, T], U8)
+        xo_s = tile("xo_s", [P, Z], U8)
+        w_s = tile("w_s", [P, R], U8)
+        w0_s = tile("w0_s", [P, R], U8)
+        wb_s = tile("wb_s", [P, N], U8)
+        xt_w = tile("xt_w", [P, T], U16)
+        xo_w = tile("xo_w", [P, Z], I32)
+        w_w = tile("w_w", [P, R], I32)
+        w0_w = tile("w0_w", [P, R], U16)
+        wb_w = tile("wb_w", [P, 2 * N], U8)
+
+        xt_st = tile("xt_st", [4, 4, T // 4], I32)
+        xo_st = tile("xo_st", [4, 4, Z // 4], I32)
+        w_st = tile("w_st", [4, 4, R // 4], I32)
+        w0_st = tile("w0_st", [4, 4, R // 4], I32)
+        for plane in (w_s, w0_s, xt_s, xo_s, wb_s):
+            nc.vector.memset(plane[:].bitcast(I32), 0)
+
+        l1 = load_list("l1", offs)
+        stage_scales(nc.scalar, xt_st, xt_scales)
+        stage_scales(nc.sync, w_st, w_scales)
+        stage_scales(nc.scalar, xo_st, xo_scales)
+        stage_scales(nc.sync, w0_st, w0_scales)
+        nc.scalar.dma_start(out=w_w[:], in_=w_words[0].rearrange("p n t -> p (n t)").bitcast(I32))
+        l2 = load_list("l2", offs2)
+        nc.scalar.dma_start(out=w0_w[:].bitcast(I32), in_=w0_words[0].bitcast(I32))
+        nc.sync.dma_start(out=xt_w[:].bitcast(I32), in_=xt_words[0].bitcast(I32))
+        nc.sync.dma_start(out=xo_w[:], in_=xo_words[0].rearrange("p n t -> p (n t)").bitcast(I32))
+        l5 = load_list("l5", offs5)
+        sg_t = load_rows(nc.sync, "sg_t", sg)
+        bg_t = load_rows(nc.sync, "bg_t", bg)
+        l3 = load_list("l3", offs3)
+        sa_t = load_rows(nc.sync, "sa_t", sa)
+        l4 = load_list("l4", offs4)
+        sb_t = load_rows(nc.sync, "sb_t", sb)
+        nc.sync.dma_start(out=wb_w[:].bitcast(I32), in_=wb_words[0].bitcast(I32))
+        l6 = load_list("l6", offs6)
+        load_scales(nc.sync, wb_s, wb_scales)
+
+        pages = [tile("page%d" % h, [P, E], F32) for h in range(N // P)]
+        for page in pages:
+            nc.vector.memset(page[:], 0.0)
+
+        w_d = tile("w_d", [P, R], U32)
+        w0_d = tile("w0_d", [P, R], U16)
+        w_sd = tile("w_sd", [P, R], U8)
+        w0_sd = tile("w0_sd", [P, R], U8)
+        deal(nc.scalar.copy, w_d[:], w_w[:].bitcast(U32), 4, slice(0, PACK))
+        deal(nc.scalar.copy, w0_d[:], w0_w[:], 8, slice(0, PACK))
+
+        for q in (3, 2, 1, 0):
+            for plane, staged in ((xt_s, xt_st), (w_s, w_st), (xo_s, xo_st), (w0_s, w0_st)):
+                nc.vector.tensor_copy(plane[32 * q : 32 * q + 4, :].bitcast(I32), staged[:, q, :])
+
+        xt_sg = tile("xt_sg", [P, J], U8)
+        xo_sg = tile("xo_sg", [P, J], U8)
+        xt_g = tile("xt_g", [P, J], U16)
+        xo_g = tile("xo_g", [P, J], U32)
+        nc.vector.tensor_copy(xt_sg[:], xt_s[:].indirect(l1[:]))
+        nc.vector.tensor_copy(xo_sg[:], xo_s[:].indirect(l2[:]))
+        deal(nc.vector.tensor_copy, w_sd[:], w_s[:], 16, slice(0, 1))
+        deal(nc.vector.tensor_copy, w0_sd[:], w0_s[:], 16, slice(0, 1))
+        nc.vector.tensor_copy(xt_g[:], xt_w[:].indirect(l1[:]))
+        nc.vector.tensor_copy(xo_g[:], xo_w[:].bitcast(U32).indirect(l2[:]))
+
+        a_ps = [psum.tile([P, J], F32, name="a_ps%d" % t) for t in range(PACK)]
+        a = [tile("a%d" % t, [P, J], F32) for t in range(PACK)]
+        for t in range(PACK):
+            cols = slice(t * P, (t + 1) * P)
+            nc.tensor.matmul_mx(
+                out=a_ps[t][:], lhsT=w_d[:, cols].bitcast(E4M3), lhsT_scale=w_sd[:, cols],
+                rhs=xt_g[:].bitcast(E2M1), rhs_scale=xt_sg[:], start=True, stop=False,
+            )
+            nc.tensor.matmul_mx(
+                out=a_ps[t][:], lhsT=w0_d[:, cols].bitcast(E2M1), lhsT_scale=w0_sd[:, cols],
+                rhs=xo_g[:].bitcast(E4M3), rhs_scale=xo_sg[:], start=False, stop=True,
+            )
+            if t == 0:
+                deal(nc.vector.tensor_copy, w_sd[:], w_s[:], 16, slice(1, PACK))
+            nc.vector.tensor_copy(a[t][:], a_ps[t][:])
+            if t == 0:
+                deal(nc.vector.tensor_copy, w0_sd[:], w0_s[:], 16, slice(1, PACK))
+
+        picks = tile("picks", [P, 1 + 2 * PACK, O], F32)
+        gate = picks[:, 0:PACK, :]
+        diff = tile("diff", [P, PACK, O], F32)
+        size = tile("size", [P, PACK, O], F32)
+        hid = tile("hid", [P, O, PACK], BF16)
+
+        def fetch_gate(t):
+            nc.scalar.activation(
+                out=gate[:, t, :], in_=a[t][:].indirect(l5[:]), func=ACT.Sigmoid,
+                bias=bg_t[:, t : t + 1], scale=sg_t[:, t : t + 1],
+            )
+
+        fetch_gate(0)
+        for t in range(PACK):
+            first, second = picks[:, 1 + 2 * t, :], picks[:, 2 + 2 * t, :]
+            nc.scalar.activation(out=first, in_=a[t][:].indirect(l3[:]), func=ACT.Copy, scale=sa_t[:, t : t + 1])
+            nc.scalar.activation(out=second, in_=a[t][:].indirect(l4[:]), func=ACT.Copy, scale=sb_t[:, t : t + 1])
+            nc.vector.tensor_tensor(diff[:, t, :], first, second, ALU.subtract)
+            nc.vector.scalar_tensor_tensor(
+                out=size[:, t, :], in0=diff[:, t, :], scalar=-1.0, in1=diff[:, t, :], op0=ALU.mult, op1=ALU.max
+            )
+        for t in range(1, PACK):
+            fetch_gate(t)
+            if t % 2 == 1:
+                pair = slice(t - 1, t + 1)
+                nc.vector.tensor_tensor(
+                    hid[:, :, pair],
+                    size[:, pair, :].rearrange("p t o -> p o t"),
+                    gate[:, pair, :].rearrange("p t o -> p o t"),
+                    ALU.mult,
+                )
+
+        hid_q = tile("hid_q", [P, O], U32)
+        hid_s = tile("hid_s", [P, O], U8)
+        nc.vector.quantize_mx(out=hid_q[:].bitcast(E5M2), scales=hid_s[:], in_=hid[:].rearrange("p o t -> p (o t)"))
+
+        p_ps = [psum.tile([P, O], F32, name="p_ps%d" % h) for h in range(N // P)]
+        p_sb = [tile("p_sb%d" % h, [P, O], F32) for h in range(N // P)]
+        for h in range(N // P):
+            nc.tensor.matmul_mx(
+                out=p_ps[h][:], lhsT=wb_w[:, 2 * P * h : 2 * P * (h + 1)].bitcast(E2M1), lhsT_scale=wb_s[:, P * h : P * (h + 1)],
+                rhs=hid_q[:].bitcast(E5M2), rhs_scale=hid_s[:], start=True, stop=True,
+            )
+        nc.scalar.copy(p_sb[0][:], p_ps[0][:])
+        nc.scalar.activation(out=pages[0][:].indirect(l6[:]), in_=p_sb[0][:], func=ACT.Copy)
+        nc.scalar.dma_start(out=out[0:P, :], in_=pages[0][:])
+        nc.vector.tensor_copy(p_sb[1][:], p_ps[1][:])
+        nc.vector.tensor_copy(pages[1][:].indirect(l6[:]), p_sb[1][:])
+        nc.sync.dma_start(out=out[P : 2 * P, :], in_=pages[1][:])

@@ -21,8 +21,8 @@ P = 128
 PACK = 4
 
 
-def stage_scales(queue, staged, scales):
-    queue.dma_start(out=staged[:], in_=scales[0].bitcast(I32).rearrange("(q r) c -> r q c", r=4))
+def stage_scales(queue, staged, rows):
+    queue.dma_start(out=staged, in_=rows.bitcast(I32))
 
 
 def load_scales(queue, plane, scales):
@@ -46,8 +46,8 @@ def tile_list_gatedlarger_bank_one_scattered_kernel(
         pool = ctx.enter_context(tc.tile_pool(name="held", bufs=1))
         psum = ctx.enter_context(tc.psum_pool(name="psum", bufs=1))
 
-        def tile(name, shape, dtype):
-            return pool.tile(shape, dtype, name=name, align_bytes=64)
+        def tile(name, shape, dtype, tag=None):
+            return pool.tile(shape, dtype, name=name, tag=tag or name, align_bytes=64)
 
         def load_list(name, source):
             t = tile(name, list(source.shape), U16)
@@ -70,37 +70,39 @@ def tile_list_gatedlarger_bank_one_scattered_kernel(
         w0_w = tile("w0_w", [P, R], U16)
         wb_w = tile("wb_w", [P, 2 * N], U8)
 
-        xt_st = tile("xt_st", [4, 4, T // 4], I32)
-        xo_st = tile("xo_st", [4, 4, Z // 4], I32)
-        w_st = tile("w_st", [4, 4, R // 4], I32)
-        w0_st = tile("w0_st", [4, 4, R // 4], I32)
-        for plane in (w_s, w0_s, xt_s, xo_s, wb_s):
+        xt_st = tile("xt_st", [P, 2, T // 4], I32)
+        xo_st = tile("xo_st", [P, 2, Z // 4], I32)
+        w_st = tile("w_st", [64, 2, R // 4], I32)
+        w0_st = tile("w0_st", [64, 2, R // 4], I32)
+        for staged in (w_st, w0_st):
+            nc.vector.memset(staged[:], 0)
+        for plane in (xt_s, xo_s, wb_s):
             nc.vector.memset(plane[:].bitcast(I32), 0)
 
+        for staged, scales in ((xt_st, xt_scales), (xo_st, xo_scales)):
+            rows = scales[0].rearrange("(h q r) c -> h r q c", h=2, q=2)
+            stage_scales(nc.sync, staged[0:4, :, :], rows[0])
+            stage_scales(nc.scalar, staged[64:68, :, :], rows[1])
         l1 = load_list("l1", offs)
-        stage_scales(nc.scalar, xt_st, xt_scales)
-        stage_scales(nc.sync, w_st, w_scales)
-        stage_scales(nc.scalar, xo_st, xo_scales)
-        stage_scales(nc.sync, w0_st, w0_scales)
         nc.scalar.dma_start(out=w_w[:], in_=w_words[0].rearrange("p n t -> p (n t)").bitcast(I32))
         l2 = load_list("l2", offs2)
         nc.scalar.dma_start(out=w0_w[:].bitcast(I32), in_=w0_words[0].bitcast(I32))
-        nc.sync.dma_start(out=xt_w[:].bitcast(I32), in_=xt_words[0].bitcast(I32))
-        nc.sync.dma_start(out=xo_w[:], in_=xo_words[0].rearrange("p n t -> p (n t)").bitcast(I32))
+        nc.scalar.dma_start(out=xt_w[:].bitcast(I32), in_=xt_words[0].bitcast(I32))
+        nc.scalar.dma_start(out=xo_w[:], in_=xo_words[0].rearrange("p n t -> p (n t)").bitcast(I32))
+        for staged, scales in ((w_st, w_scales), (w0_st, w0_scales)):
+            rows = scales[0].rearrange("(h q r) c -> q r h c", h=2, q=2)
+            for q in range(2):
+                stage_scales(nc.sync, staged[32 * q : 32 * q + 4, :, :], rows[q])
         l5 = load_list("l5", offs5)
         sg_t = load_rows(nc.sync, "sg_t", sg)
         bg_t = load_rows(nc.sync, "bg_t", bg)
         l3 = load_list("l3", offs3)
-        sa_t = load_rows(nc.sync, "sa_t", sa)
+        sa_t = load_rows(nc.gpsimd, "sa_t", sa)
         l4 = load_list("l4", offs4)
-        sb_t = load_rows(nc.sync, "sb_t", sb)
-        nc.sync.dma_start(out=wb_w[:].bitcast(I32), in_=wb_words[0].bitcast(I32))
+        sb_t = load_rows(nc.gpsimd, "sb_t", sb)
         l6 = load_list("l6", offs6)
+        nc.sync.dma_start(out=wb_w[:].bitcast(I32), in_=wb_words[0].bitcast(I32))
         load_scales(nc.sync, wb_s, wb_scales)
-
-        pages = [tile("page%d" % h, [P, E], F32) for h in range(N // P)]
-        for page in pages:
-            nc.vector.memset(page[:], 0.0)
 
         w_d = tile("w_d", [P, R], U32)
         w0_d = tile("w0_d", [P, R], U16)
@@ -110,8 +112,9 @@ def tile_list_gatedlarger_bank_one_scattered_kernel(
         deal(nc.scalar.copy, w0_d[:], w0_w[:], 8, slice(0, PACK))
 
         for q in (3, 2, 1, 0):
-            for plane, staged in ((xt_s, xt_st), (w_s, w_st), (xo_s, xo_st), (w0_s, w0_st)):
-                nc.vector.tensor_copy(plane[32 * q : 32 * q + 4, :].bitcast(I32), staged[:, q, :])
+            source = 64 * (q // 2)
+            for plane, staged in ((xt_s, xt_st), (xo_s, xo_st)):
+                nc.vector.tensor_copy(plane[32 * q : 32 * q + 4, :].bitcast(I32), staged[source : source + 4, q % 2, :])
 
         xt_sg = tile("xt_sg", [P, J], U8)
         xo_sg = tile("xo_sg", [P, J], U8)
@@ -119,6 +122,9 @@ def tile_list_gatedlarger_bank_one_scattered_kernel(
         xo_g = tile("xo_g", [P, J], U32)
         nc.vector.tensor_copy(xt_sg[:], xt_s[:].indirect(l1[:]))
         nc.vector.tensor_copy(xo_sg[:], xo_s[:].indirect(l2[:]))
+        for h in (1, 0):
+            for plane, staged in ((w_s, w_st), (w0_s, w0_st)):
+                nc.vector.tensor_copy(plane[64 * h : 64 * h + 64, :].bitcast(I32), staged[:, h, :])
         deal(nc.vector.tensor_copy, w_sd[:], w_s[:], 16, slice(0, 1))
         deal(nc.vector.tensor_copy, w0_sd[:], w0_s[:], 16, slice(0, 1))
         nc.vector.tensor_copy(xt_g[:], xt_w[:].indirect(l1[:]))
@@ -137,10 +143,16 @@ def tile_list_gatedlarger_bank_one_scattered_kernel(
                 rhs=xo_g[:].bitcast(E4M3), rhs_scale=xo_sg[:], start=False, stop=True,
             )
             if t == 0:
-                deal(nc.vector.tensor_copy, w_sd[:], w_s[:], 16, slice(1, PACK))
+                deal(nc.vector.tensor_copy, w_sd[:], w_s[:], 16, slice(1, 2))
+                deal(nc.vector.tensor_copy, w0_sd[:], w0_s[:], 16, slice(1, 2))
             nc.vector.tensor_copy(a[t][:], a_ps[t][:])
             if t == 0:
-                deal(nc.vector.tensor_copy, w0_sd[:], w0_s[:], 16, slice(1, PACK))
+                deal(nc.vector.tensor_copy, w_sd[:], w_s[:], 16, slice(2, PACK))
+                deal(nc.vector.tensor_copy, w0_sd[:], w0_s[:], 16, slice(2, PACK))
+
+        pages = [tile("page0", [P, E], F32, tag="w_s"), tile("page1", [P, E], F32, tag="w0_s")]
+        for page in pages:
+            nc.gpsimd.memset(page[:], 0.0)
 
         picks = tile("picks", [P, 1 + 2 * PACK, O], F32)
         gate = picks[:, 0:PACK, :]

@@ -32,7 +32,7 @@ def load_scales(queue, plane, scales):
 
 def deal(copy, dealt, raw, run, slots):
     copy(
-        out=dealt.rearrange("p (t b i) -> p b t i", t=PACK, i=run)[:, :, slots, :],
+        out=dealt.rearrange("p (t b i) -> p b t i", b=P // run, i=run),
         in_=raw.rearrange("p (b i t) -> p b t i", t=PACK, i=run)[:, :, slots, :],
     )
 
@@ -72,27 +72,23 @@ def tile_list_gatedlarger_bank_one_scattered_kernel(
 
         xt_st = tile("xt_st", [P, 2, T // 4], I32)
         xo_st = tile("xo_st", [P, 2, Z // 4], I32)
-        w_st = tile("w_st", [64, 2, R // 4], I32)
-        w0_st = tile("w0_st", [64, 2, R // 4], I32)
-        for staged in (w_st, w0_st):
-            nc.vector.memset(staged[:], 0)
-        for plane in (xt_s, xo_s, wb_s):
+        w_st = tile("w_st", [4, 4, R // 4], I32)
+        w0_st = tile("w0_st", [4, 4, R // 4], I32)
+        for plane in (xt_s, xo_s, w_s, w0_s, wb_s):
             nc.vector.memset(plane[:].bitcast(I32), 0)
 
         for staged, scales in ((xt_st, xt_scales), (xo_st, xo_scales)):
             rows = scales[0].rearrange("(h q r) c -> h r q c", h=2, q=2)
             stage_scales(nc.sync, staged[0:4, :, :], rows[0])
             stage_scales(nc.scalar, staged[64:68, :, :], rows[1])
-        l1 = load_list("l1", offs)
-        nc.scalar.dma_start(out=w_w[:], in_=w_words[0].rearrange("p n t -> p (n t)").bitcast(I32))
-        l2 = load_list("l2", offs2)
+        stage_scales(nc.sync, w_st[:], w_scales[0].rearrange("(q r) c -> r q c", r=4))
+        stage_scales(nc.scalar, w0_st[:], w0_scales[0].rearrange("(q r) c -> r q c", r=4))
+        nc.sync.dma_start(out=w_w[:], in_=w_words[0].rearrange("p n t -> p (n t)").bitcast(I32))
         nc.scalar.dma_start(out=w0_w[:].bitcast(I32), in_=w0_words[0].bitcast(I32))
-        nc.scalar.dma_start(out=xt_w[:].bitcast(I32), in_=xt_words[0].bitcast(I32))
-        nc.scalar.dma_start(out=xo_w[:], in_=xo_words[0].rearrange("p n t -> p (n t)").bitcast(I32))
-        for staged, scales in ((w_st, w_scales), (w0_st, w0_scales)):
-            rows = scales[0].rearrange("(h q r) c -> q r h c", h=2, q=2)
-            for q in range(2):
-                stage_scales(nc.sync, staged[32 * q : 32 * q + 4, :, :], rows[q])
+        l1 = load_list("l1", offs)
+        l2 = load_list("l2", offs2)
+        nc.sync.dma_start(out=xt_w[:].bitcast(I32), in_=xt_words[0].bitcast(I32))
+        nc.sync.dma_start(out=xo_w[:], in_=xo_words[0].rearrange("p n t -> p (n t)").bitcast(I32))
         l5 = load_list("l5", offs5)
         sg_t = load_rows(nc.sync, "sg_t", sg)
         bg_t = load_rows(nc.sync, "bg_t", bg)
@@ -106,8 +102,8 @@ def tile_list_gatedlarger_bank_one_scattered_kernel(
 
         w_d = tile("w_d", [P, R], U32)
         w0_d = tile("w0_d", [P, R], U16)
-        w_sd = tile("w_sd", [P, R], U8)
-        w0_sd = tile("w0_sd", [P, R], U8)
+        w_sd = tile("w_sd", [P, P], U8)
+        w0_sd = tile("w0_sd", [P, P], U8)
         deal(nc.scalar.copy, w_d[:], w_w[:].bitcast(U32), 4, slice(0, PACK))
         deal(nc.scalar.copy, w0_d[:], w0_w[:], 8, slice(0, PACK))
 
@@ -116,41 +112,46 @@ def tile_list_gatedlarger_bank_one_scattered_kernel(
             for plane, staged in ((xt_s, xt_st), (xo_s, xo_st)):
                 nc.vector.tensor_copy(plane[32 * q : 32 * q + 4, :].bitcast(I32), staged[source : source + 4, q % 2, :])
 
+        for q in (3, 2, 1, 0):
+            for plane, staged in ((w_s, w_st), (w0_s, w0_st)):
+                nc.vector.tensor_copy(plane[32 * q : 32 * q + 4, :].bitcast(I32), staged[:, q, :])
+
         xt_sg = tile("xt_sg", [P, J], U8)
         xo_sg = tile("xo_sg", [P, J], U8)
         xt_g = tile("xt_g", [P, J], U16)
         xo_g = tile("xo_g", [P, J], U32)
         nc.vector.tensor_copy(xt_sg[:], xt_s[:].indirect(l1[:]))
         nc.vector.tensor_copy(xo_sg[:], xo_s[:].indirect(l2[:]))
-        for h in (1, 0):
-            for plane, staged in ((w_s, w_st), (w0_s, w0_st)):
-                nc.vector.tensor_copy(plane[64 * h : 64 * h + 64, :].bitcast(I32), staged[:, h, :])
         deal(nc.vector.tensor_copy, w_sd[:], w_s[:], 16, slice(0, 1))
         deal(nc.vector.tensor_copy, w0_sd[:], w0_s[:], 16, slice(0, 1))
         nc.vector.tensor_copy(xt_g[:], xt_w[:].indirect(l1[:]))
         nc.vector.tensor_copy(xo_g[:], xo_w[:].bitcast(U32).indirect(l2[:]))
 
+        second_sd = tile("second_sd", [P, 2, P], U8, tag="xo_w")
+        last_sd = tile("last_sd", [P, 2, 2 * P], U8, tag="w0_sd")
+        w_planes = [w_sd[:], second_sd[:, 0, :], last_sd[:, 0, :P], last_sd[:, 0, P:]]
+        w0_planes = [w0_sd[:], second_sd[:, 1, :], last_sd[:, 1, :P], last_sd[:, 1, P:]]
         a_ps = [psum.tile([P, J], F32, name="a_ps%d" % t) for t in range(PACK)]
         a = [tile("a%d" % t, [P, J], F32) for t in range(PACK)]
         for t in range(PACK):
             cols = slice(t * P, (t + 1) * P)
             nc.tensor.matmul_mx(
-                out=a_ps[t][:], lhsT=w_d[:, cols].bitcast(E4M3), lhsT_scale=w_sd[:, cols],
+                out=a_ps[t][:], lhsT=w_d[:, cols].bitcast(E4M3), lhsT_scale=w_planes[t],
                 rhs=xt_g[:].bitcast(E2M1), rhs_scale=xt_sg[:], start=True, stop=False,
             )
             nc.tensor.matmul_mx(
-                out=a_ps[t][:], lhsT=w0_d[:, cols].bitcast(E2M1), lhsT_scale=w0_sd[:, cols],
+                out=a_ps[t][:], lhsT=w0_d[:, cols].bitcast(E2M1), lhsT_scale=w0_planes[t],
                 rhs=xo_g[:].bitcast(E4M3), rhs_scale=xo_sg[:], start=False, stop=True,
             )
             if t == 0:
-                deal(nc.vector.tensor_copy, w_sd[:], w_s[:], 16, slice(1, 2))
-                deal(nc.vector.tensor_copy, w0_sd[:], w0_s[:], 16, slice(1, 2))
+                deal(nc.vector.tensor_copy, second_sd[:, 0, :], w_s[:], 16, slice(1, 2))
+                deal(nc.vector.tensor_copy, second_sd[:, 1, :], w0_s[:], 16, slice(1, 2))
             nc.vector.tensor_copy(a[t][:], a_ps[t][:])
             if t == 0:
-                deal(nc.vector.tensor_copy, w_sd[:], w_s[:], 16, slice(2, PACK))
-                deal(nc.vector.tensor_copy, w0_sd[:], w0_s[:], 16, slice(2, PACK))
+                deal(nc.vector.tensor_copy, last_sd[:, 0, :], w_s[:], 16, slice(2, PACK))
+                deal(nc.vector.tensor_copy, last_sd[:, 1, :], w0_s[:], 16, slice(2, PACK))
 
-        pages = [tile("page0", [P, E], F32, tag="w_s"), tile("page1", [P, E], F32, tag="w0_s")]
+        pages = [tile("page0", [P, E], F32, tag="w_d"), tile("page1", [P, E], F32, tag="w0_d")]
         for page in pages:
             nc.gpsimd.memset(page[:], 0.0)
 
@@ -166,8 +167,7 @@ def tile_list_gatedlarger_bank_one_scattered_kernel(
                 bias=bg_t[:, t : t + 1], scale=sg_t[:, t : t + 1],
             )
 
-        fetch_gate(0)
-        for t in range(PACK):
+        def fetch_size(t):
             first, second = picks[:, 1 + 2 * t, :], picks[:, 2 + 2 * t, :]
             nc.scalar.activation(out=first, in_=a[t][:].indirect(l3[:]), func=ACT.Copy, scale=sa_t[:, t : t + 1])
             nc.scalar.activation(out=second, in_=a[t][:].indirect(l4[:]), func=ACT.Copy, scale=sb_t[:, t : t + 1])
@@ -175,16 +175,25 @@ def tile_list_gatedlarger_bank_one_scattered_kernel(
             nc.vector.scalar_tensor_tensor(
                 out=size[:, t, :], in0=diff[:, t, :], scalar=-1.0, in1=diff[:, t, :], op0=ALU.mult, op1=ALU.max
             )
-        for t in range(1, PACK):
-            fetch_gate(t)
-            if t % 2 == 1:
-                pair = slice(t - 1, t + 1)
-                nc.vector.tensor_tensor(
-                    hid[:, :, pair],
-                    size[:, pair, :].rearrange("p t o -> p o t"),
-                    gate[:, pair, :].rearrange("p t o -> p o t"),
-                    ALU.mult,
-                )
+
+        def join(pair):
+            nc.vector.tensor_tensor(
+                hid[:, :, pair],
+                size[:, pair, :].rearrange("p t o -> p o t"),
+                gate[:, pair, :].rearrange("p t o -> p o t"),
+                ALU.mult,
+            )
+
+        fetch_gate(0)
+        fetch_size(0)
+        fetch_size(1)
+        fetch_gate(1)
+        join(slice(0, 2))
+        fetch_size(2)
+        fetch_size(3)
+        fetch_gate(2)
+        fetch_gate(3)
+        join(slice(2, 4))
 
         hid_q = tile("hid_q", [P, O], U32)
         hid_s = tile("hid_s", [P, O], U8)
@@ -198,8 +207,8 @@ def tile_list_gatedlarger_bank_one_scattered_kernel(
                 rhs=hid_q[:].bitcast(E5M2), rhs_scale=hid_s[:], start=True, stop=True,
             )
         nc.scalar.copy(p_sb[0][:], p_ps[0][:])
-        nc.scalar.activation(out=pages[0][:].indirect(l6[:]), in_=p_sb[0][:], func=ACT.Copy)
-        nc.scalar.dma_start(out=out[0:P, :], in_=pages[0][:])
         nc.vector.tensor_copy(p_sb[1][:], p_ps[1][:])
-        nc.vector.tensor_copy(pages[1][:].indirect(l6[:]), p_sb[1][:])
-        nc.sync.dma_start(out=out[P : 2 * P, :], in_=pages[1][:])
+        nc.vector.tensor_copy(pages[0][:].indirect(l6[:]), p_sb[0][:])
+        nc.scalar.activation(out=pages[1][:].indirect(l6[:]), in_=p_sb[1][:], func=ACT.Copy)
+        nc.sync.dma_start(out=out[0:P, :], in_=pages[0][:])
+        nc.scalar.dma_start(out=out[P : 2 * P, :], in_=pages[1][:])

from contextlib import ExitStack

import concourse.mybir as mybir

K, T, J, R, F, Z, O, N, E = 512, 1024, 256, 512, 512, 1024, 128, 256, 1024
FLOPS = 2 * (K * R * J + F * R * J + R * N * O)

F32 = mybir.dt.float32
BF16 = mybir.dt.bfloat16
I32 = mybir.dt.int32
U32 = mybir.dt.uint32
U16 = mybir.dt.uint16
U8 = mybir.dt.uint8
E4M3 = mybir.dt.float8_e4m3fn_x4
E5M2 = mybir.dt.float8_e5m2_x4
E2M1 = mybir.dt.float4_e2m1fn_x4
ACT = mybir.ActivationFunctionType
ALU = mybir.AluOpType

P = 128
PACK = 4


def stage_scales(queue, staged, rows):
    queue.dma_start(out=staged, in_=rows.bitcast(I32))


def load_scales(queue, plane, scales):
    for q in range(4):
        queue.dma_start(out=plane[32 * q : 32 * q + 4, :].bitcast(I32), in_=scales[0, 4 * q : 4 * q + 4, :].bitcast(I32))


def deal(copy, dealt, raw, run, slots):
    copy(
        out=dealt.rearrange("p (t b i) -> p b t i", b=P // run, i=run),
        in_=raw.rearrange("p (b i t) -> p b t i", t=PACK, i=run)[:, :, slots, :],
    )


def tile_list_gatedlarger_bank_one_scattered_kernel(
    tc, xt_words, xt_scales, xo_words, xo_scales, w_words, w_scales, w0_words, w0_scales,
    sa, sb, sg, bg, wb_words, wb_scales, offs, offs2, offs3, offs4, offs5, offs6, out,
):
    nc = tc.nc
    with ExitStack() as ctx:
        pool = ctx.enter_context(tc.tile_pool(name="held", bufs=1))
        psum = ctx.enter_context(tc.psum_pool(name="psum", bufs=1))

        def tile(name, shape, dtype, tag=None):
            return pool.tile(shape, dtype, name=name, tag=tag or name, align_bytes=64)

        def load_list(name, source):
            t = tile(name, list(source.shape), U16)
            nc.sync.dma_start(t[:], source)
            return t

        def load_rows(queue, name, source):
            t = tile(name, [P, PACK], F32)
            queue.dma_start(out=t[:], in_=source.rearrange("(p t) o -> p (t o)", t=PACK))
            return t

        xt_s = tile("xt_s", [P, T], U8)
        xo_s = tile("xo_s", [P, Z], U8)
        w_s = tile("w_s", [P, R], U8)
        w0_s = tile("w0_s", [P, R], U8)
        wb_s = tile("wb_s", [P, N], U8)
        xt_w = tile("xt_w", [P, T], U16)
        xo_w = tile("xo_w", [P, Z], I32)
        w_w = tile("w_w", [P, R], I32)
        w0_w = tile("w0_w", [P, R], U16)
        wb_w = tile("wb_w", [P, 2 * N], U8)

        xt_st = tile("xt_st", [P, 2, T // 4], I32)
        xo_st = tile("xo_st", [P, 2, Z // 4], I32)
        w_st = tile("w_st", [4, 4, R // 4], I32)
        w0_st = tile("w0_st", [4, 4, R // 4], I32)
        for plane in (xt_s, xo_s, w_s, w0_s, wb_s):
            nc.vector.memset(plane[:].bitcast(I32), 0)

        for staged, scales in ((xt_st, xt_scales), (xo_st, xo_scales)):
            rows = scales[0].rearrange("(h q r) c -> h r q c", h=2, q=2)
            stage_scales(nc.sync, staged[0:4, :, :], rows[0])
            stage_scales(nc.scalar, staged[64:68, :, :], rows[1])
        stage_scales(nc.sync, w_st[:], w_scales[0].rearrange("(q r) c -> r q c", r=4))
        stage_scales(nc.scalar, w0_st[:], w0_scales[0].rearrange("(q r) c -> r q c", r=4))
        nc.sync.dma_start(out=w_w[:], in_=w_words[0].rearrange("p n t -> p (n t)").bitcast(I32))
        nc.scalar.dma_start(out=w0_w[:].bitcast(I32), in_=w0_words[0].bitcast(I32))
        l1 = load_list("l1", offs)
        l2 = load_list("l2", offs2)
        nc.sync.dma_start(out=xt_w[:].bitcast(I32), in_=xt_words[0].bitcast(I32))
        nc.sync.dma_start(out=xo_w[:], in_=xo_words[0].rearrange("p n t -> p (n t)").bitcast(I32))
        l5 = load_list("l5", offs5)
        sg_t = load_rows(nc.sync, "sg_t", sg)
        bg_t = load_rows(nc.sync, "bg_t", bg)
        l3 = load_list("l3", offs3)
        sa_t = load_rows(nc.gpsimd, "sa_t", sa)
        l4 = load_list("l4", offs4)
        sb_t = load_rows(nc.gpsimd, "sb_t", sb)
        l6 = load_list("l6", offs6)
        nc.sync.dma_start(out=wb_w[:].bitcast(I32), in_=wb_words[0].bitcast(I32))
        load_scales(nc.sync, wb_s, wb_scales)

        w_d = tile("w_d", [P, R], U32)
        w0_d = tile("w0_d", [P, R], U16)
        w_sd = tile("w_sd", [P, P], U8)
        w0_sd = tile("w0_sd", [P, P], U8)
        deal(nc.scalar.copy, w_d[:], w_w[:].bitcast(U32), 4, slice(0, PACK))
        deal(nc.scalar.copy, w0_d[:], w0_w[:], 8, slice(0, PACK))

        for q in (3, 2, 1, 0):
            source = 64 * (q // 2)
            for plane, staged in ((xt_s, xt_st), (xo_s, xo_st)):
                nc.vector.tensor_copy(plane[32 * q : 32 * q + 4, :].bitcast(I32), staged[source : source + 4, q % 2, :])

        for q in (3, 2, 1, 0):
            for plane, staged in ((w_s, w_st), (w0_s, w0_st)):
                nc.vector.tensor_copy(plane[32 * q : 32 * q + 4, :].bitcast(I32), staged[:, q, :])

        xt_sg = tile("xt_sg", [P, J], U8)
        xo_sg = tile("xo_sg", [P, J], U8)
        xt_g = tile("xt_g", [P, J], U16)
        xo_g = tile("xo_g", [P, J], U32)
        nc.vector.tensor_copy(xt_sg[:], xt_s[:].indirect(l1[:]))
        nc.vector.tensor_copy(xo_sg[:], xo_s[:].indirect(l2[:]))
        deal(nc.vector.tensor_copy, w_sd[:], w_s[:], 16, slice(0, 1))
        deal(nc.vector.tensor_copy, w0_sd[:], w0_s[:], 16, slice(0, 1))
        nc.vector.tensor_copy(xt_g[:], xt_w[:].indirect(l1[:]))
        nc.vector.tensor_copy(xo_g[:], xo_w[:].bitcast(U32).indirect(l2[:]))

        second_sd = tile("second_sd", [P, 2, P], U8, tag="xo_w")
        last_sd = tile("last_sd", [P, 2, 2 * P], U8, tag="w0_sd")
        w_planes = [w_sd[:], second_sd[:, 0, :], last_sd[:, 0, :P], last_sd[:, 0, P:]]
        w0_planes = [w0_sd[:], second_sd[:, 1, :], last_sd[:, 1, :P], last_sd[:, 1, P:]]
        a_ps = [psum.tile([P, J], F32, name="a_ps%d" % t) for t in range(PACK)]
        a = [tile("a%d" % t, [P, J], F32) for t in range(PACK)]
        for t in range(PACK):
            cols = slice(t * P, (t + 1) * P)
            nc.tensor.matmul_mx(
                out=a_ps[t][:], lhsT=w_d[:, cols].bitcast(E4M3), lhsT_scale=w_planes[t],
                rhs=xt_g[:].bitcast(E2M1), rhs_scale=xt_sg[:], start=True, stop=False,
            )
            nc.tensor.matmul_mx(
                out=a_ps[t][:], lhsT=w0_d[:, cols].bitcast(E2M1), lhsT_scale=w0_planes[t],
                rhs=xo_g[:].bitcast(E4M3), rhs_scale=xo_sg[:], start=False, stop=True,
            )
            if t == 0:
                deal(nc.vector.tensor_copy, second_sd[:, 0, :], w_s[:], 16, slice(1, 2))
                deal(nc.vector.tensor_copy, second_sd[:, 1, :], w0_s[:], 16, slice(1, 2))
            nc.vector.tensor_copy(a[t][:], a_ps[t][:])
            if t == 0:
                deal(nc.vector.tensor_copy, last_sd[:, 0, :], w_s[:], 16, slice(2, PACK))
                deal(nc.vector.tensor_copy, last_sd[:, 1, :], w0_s[:], 16, slice(2, PACK))

        pages = [tile("page0", [P, E], F32, tag="w_d"), tile("page1", [P, E], F32, tag="w0_d")]
        for page in pages:
            nc.gpsimd.memset(page[:], 0.0)

        picks = tile("picks", [P, 1 + 2 * PACK, O], F32)
        gate = picks[:, 0:PACK, :]
        diff = tile("diff", [P, PACK, O], F32)
        size = tile("size", [P, PACK, O], F32)
        hid = tile("hid", [P, O, PACK], BF16)

        def fetch_gate(t):
            nc.scalar.activation(
                out=gate[:, t, :], in_=a[t][:].indirect(l5[:]), func=ACT.Sigmoid,
                bias=bg_t[:, t : t + 1], scale=sg_t[:, t : t + 1],
            )

        def fetch_size(t):
            first, second = picks[:, 1 + 2 * t, :], picks[:, 2 + 2 * t, :]
            nc.scalar.activation(out=first, in_=a[t][:].indirect(l3[:]), func=ACT.Copy, scale=sa_t[:, t : t + 1])
            nc.scalar.activation(out=second, in_=a[t][:].indirect(l4[:]), func=ACT.Copy, scale=sb_t[:, t : t + 1])
            nc.vector.tensor_tensor(diff[:, t, :], first, second, ALU.subtract)
            nc.vector.scalar_tensor_tensor(
                out=size[:, t, :], in0=diff[:, t, :], scalar=-1.0, in1=diff[:, t, :], op0=ALU.mult, op1=ALU.max
            )

        def join(pair):
            nc.vector.tensor_tensor(
                hid[:, :, pair],
                size[:, pair, :].rearrange("p t o -> p o t"),
                gate[:, pair, :].rearrange("p t o -> p o t"),
                ALU.mult,
            )

        fetch_gate(0)
        fetch_size(0)
        fetch_size(1)
        fetch_gate(1)
        join(slice(0, 2))
        fetch_size(2)
        fetch_size(3)
        fetch_gate(2)
        fetch_gate(3)
        join(slice(2, 4))

        hid_q = tile("hid_q", [P, O], U32)
        hid_s = tile("hid_s", [P, O], U8)
        nc.vector.quantize_mx(out=hid_q[:].bitcast(E5M2), scales=hid_s[:], in_=hid[:].rearrange("p o t -> p (o t)"))

        p_ps = [psum.tile([P, O], F32, name="p_ps%d" % h) for h in range(N // P)]
        p_sb = [tile("p_sb%d" % h, [P, O], F32) for h in range(N // P)]
        for h in range(N // P):
            nc.tensor.matmul_mx(
                out=p_ps[h][:], lhsT=wb_w[:, 2 * P * h : 2 * P * (h + 1)].bitcast(E2M1), lhsT_scale=wb_s[:, P * h : P * (h + 1)],
                rhs=hid_q[:].bitcast(E5M2), rhs_scale=hid_s[:], start=True, stop=True,
            )
        nc.scalar.copy(p_sb[0][:], p_ps[0][:])
        nc.vector.tensor_copy(p_sb[1][:], p_ps[1][:])
        nc.vector.tensor_copy(pages[0][:].indirect(l6[:]), p_sb[0][:])
        nc.scalar.activation(out=pages[1][:].indirect(l6[:]), in_=p_sb[1][:], func=ACT.Copy)
        nc.sync.dma_start(out=out[0:P, :], in_=pages[0][:])
        nc.scalar.dma_start(out=out[P : 2 * P, :], in_=pages[1][:])
